import numpy as np
import ml_dtypes


def mxq(x, axis, fmt="e4m3"):
    dtype, down = {"e4m3": (ml_dtypes.float8_e4m3fn, 7), "e5m2": (ml_dtypes.float8_e5m2, 14)}[fmt]
    v = np.moveaxis(np.asarray(x, np.float32).astype(ml_dtypes.bfloat16).astype(np.float64), axis, -1)
    blocks = v.reshape(v.shape[:-1] + (-1, 32))
    amax = np.abs(blocks).max(-1, keepdims=True)
    byte = np.maximum(np.where(amax > 0, np.frexp(amax)[1] - 1 + 127, 0) - down, 1)
    scale = np.exp2(byte - 127.0)
    codes = (blocks / scale).astype(np.float32).astype(dtype).astype(np.float64)
    return np.moveaxis((codes * scale).reshape(v.shape), -1, axis)


WIDE = False


def mx_kscale(k, group=512):
    if not WIDE:
        return np.ones(k)
    levels = np.array([10, -10, 5, -5, 0])
    if group != 512:
        return np.exp2(np.random.permutation(np.resize(levels, k // group))).repeat(group)
    if k % 512:
        return np.exp2(np.random.permutation(np.resize(levels, k // 32))).repeat(32)
    a = np.empty((k // 512, 16))
    for p in range(k // 512):
        a[p, :8] = np.random.permutation(np.resize(levels, 8))
        for g in range(8):
            far = levels[np.abs(levels - a[p, g]) >= 10]
            a[p, g + 8] = far[np.random.randint(len(far))]
    return np.exp2(a.ravel()).repeat(32)


def f64(x):
    return np.asarray(x).astype(np.float64)


def striped(idx):
    return np.tile(np.asarray(idx).reshape(-1, 16).T, (8, 1)).astype(np.uint16)


def unstriped(offs):
    return offs[:16].T.reshape(-1).astype(np.int64)


H, KV, D, NQ, N = 4, 4, 256, 512, 512


def setup_inputs():
    n = np.random.standard_normal
    s = mx_kscale(D, 0)[:, None]
    u = mx_kscale(N)
    t = np.random.uniform(0.5, 2.0, N) * u
    v = n((KV, N, 128))
    return {
        "qT": (n((H, D, NQ)) * s * (0.70 / np.sqrt(D))).astype(np.float32),
        "kT": (n((KV, D, N)) / s).astype(np.float32),
        "t": t.reshape(N, 1).astype(np.float32),
        "v": (v / t[:, None]).astype(np.float32),
        "mask": np.exp2(-np.abs(np.arange(NQ)[None, :] * N / NQ - np.arange(N)[:, None]) / 256.0).astype(np.float32),
        "og": n((H, NQ, 128)).astype(np.float32),
    }


def reference(qT, kT, t, v, mask, og):
    a = mxq(f64(kT), 1, "e4m3").transpose(0, 2, 1) @ mxq(f64(qT), 1, "e4m3")
    p = a
    p = p * f64(mask)
    w = p * f64(t)
    y = mxq(w, 1, "e4m3").transpose(0, 2, 1) @ mxq(f64(v), 1, "e4m3")
    y = y / 16.0
    y = y / (1.0 + np.exp(-f64(og)))
    return y

@@ -1,0 +1,293 @@
+from contextlib import ExitStack
+
+import concourse.mybir as mybir
+
+H, D, NQ, N, E = 4, 256, 512, 512, 128
+FLOPS = 2 * H * N * NQ * D + 2 * H * N * NQ * E
+
+F32 = mybir.dt.float32
+BF16 = mybir.dt.bfloat16
+U32 = mybir.dt.uint32
+U8 = mybir.dt.uint8
+FP8X4 = mybir.dt.float8_e4m3fn_x4
+MULT = mybir.AluOpType.mult
+ACT = mybir.ActivationFunctionType
+
+P = 128
+ROWS = 64
+HALF = 256
+K_SPLIT = 84
+Q_SPLIT = 80
+EARLY = 8
+
+
+def tile_rows_a_lin_mask_gate_kernel(tc, qT, kT, t, v, mask, og, out):
+    nc = tc.nc
+    q_rows = qT.rearrange("h d w -> (h d) w")
+    k_rows = kT.rearrange("h d w -> (h d) w")
+
+    with ExitStack() as ctx:
+        sb = ctx.enter_context(tc.tile_pool(name="sb", bufs=1))
+        ps = ctx.enter_context(tc.psum_pool(name="ps", bufs=1))
+        ctx.enter_context(tc.manual_schedule())
+
+        def tile(name, shape, dtype):
+            return sb.tile(shape, dtype, name=name, align_bytes=64)
+
+        def mx_tiles(name, words):
+            return (
+                tile(name + "_bf", [P, words * 4], BF16),
+                tile(name + "_codes", [P, words], U32),
+                tile(name + "_scales", [P, words], U8),
+            )
+
+        score_banks = [[ps.tile([P, 4, P], F32, name="score%d_%d" % (hh, i)) for i in range(3)] for hh in range(2)]
+        y_banks = [ps.tile([P, 4, E], F32, name="y%d" % i) for i in range(2)]
+
+        t_sb = tile("t_sb", [P, 4], F32)
+        og_first = tile("og_first", [P, EARLY], F32)
+        k_raw = [[tile("k_raw0", [P, 4, N], F32)], [tile("k_raw1_%d" % i, [P, 4, HALF], F32) for i in range(2)]]
+        q_raw = [[tile("q_raw%d%d" % (a, g), [P, 4, HALF], F32) for g in range(2)] for a in range(2)]
+        m_raw = [tile("m_raw%d" % g, [P, 4, HALF], F32) for g in range(2)]
+        v_raw = [tile("v_raw%d" % a, [P, 2, 4 * E], F32) for a in range(2)]
+        og_raw = [[tile("og_raw%d%d" % (a, g), [P, 2, 2 * E], F32) for g in range(2)] for a in range(2)]
+        gate = [[tile("gate%d%d" % (a, g), [P, 2, 2 * E], F32) for g in range(2)] for a in range(2)]
+        res = [[tile("res%d%d" % (a, g), [P, 2, 2 * E], F32) for g in range(2)] for a in range(2)]
+        mt = [[tile("mt%d%d" % (g, c), [P, 4, P], F32) for c in range(2)] for g in range(2)]
+        k_mx = [mx_tiles("k%d" % a, N) for a in range(2)]
+        q_mx = [[mx_tiles("q%d%d" % (a, g), HALF) for g in range(2)] for a in range(2)]
+        v_mx = [mx_tiles("v%d" % a, 2 * E) for a in range(2)]
+        w_mx = [mx_tiles("w%d" % u, 2 * P) for u in range(8)]
+
+        def unit(u):
+            return u // 4, (u // 2) % 2, u % 2
+
+        def load_k(a, i):
+            raw = k_raw[a][i]
+            width = raw.shape[2]
+            src = k_rows[512 * a : 512 * (a + 1), width * i : width * (i + 1)]
+            nc.sync.dma_start(out=raw[:], in_=src.rearrange("(p j) w -> p j w", j=4))
+
+        def load_q(a, g):
+            src = q_rows[512 * a : 512 * (a + 1), HALF * g : HALF * (g + 1)]
+            nc.sync.dma_start(out=q_raw[a][g][:], in_=src.rearrange("(p j) w -> p j w", j=4))
+
+        def load_mask(g):
+            src = mask[:, HALF * g : HALF * (g + 1)]
+            nc.sync.dma_start(out=m_raw[g][:], in_=src.rearrange("(p r) w -> p r w", r=4))
+
+        def load_v(a):
+            nc.sync.dma_start(out=v_raw[a][:], in_=v[2 * a : 2 * a + 2].rearrange("h (p r) e -> p h (r e)", r=4))
+
+        def rows_of(x, a, g):
+            return x[2 * a : 2 * a + 2, HALF * g : HALF * (g + 1), :].rearrange("h (p c) e -> p h (c e)", c=2)
+
+        def load_og(a, g):
+            nc.sync.dma_start(out=og_raw[a][g][:], in_=rows_of(og, a, g))
+
+        def copy_on(eng, dst, src):
+            if eng == "vector":
+                nc.vector.tensor_copy(out=dst, in_=src)
+            else:
+                nc.scalar.copy(out=dst, in_=src)
+
+        def cast_k(eng, a, i, s0, s1):
+            raw = k_raw[a][i]
+            base = i * raw.shape[2] // 4
+            dst = k_mx[a][0][:].rearrange("p (rr rl s j) -> p rr s j rl", rr=2, rl=2, j=4)
+            src = raw[:].rearrange("p j (s rr rl) -> p rr s j rl", rr=2, rl=2)
+            copy_on(eng, dst[:, :, base + s0 : base + s1], src[:, :, s0:s1])
+
+        def cast_q(eng, a, g, s0, s1):
+            dst = q_mx[a][g][0][:].rearrange("p (c s j) -> p s j c", c=2, j=4)
+            src = q_raw[a][g][:].rearrange("p j (s c) -> p s j c", c=2)
+            copy_on(eng, dst[:, s0:s1], src[:, s0:s1])
+
+        def cast_v(a):
+            dst = v_mx[a][0][:].rearrange("p (h e i r) -> p h e r i", h=2, i=2, r=4)
+            src = v_raw[a][:].rearrange("p h (r e i) -> p h e r i", r=4, i=2)
+            nc.scalar.copy(out=dst, in_=src)
+
+        def quantize(mx, w0=0, w1=None):
+            values, codes, scales = mx
+            w1 = codes.shape[1] if w1 is None else w1
+            nc.vector.quantize_mx(
+                out=codes[:, w0:w1].bitcast(FP8X4), scales=scales[:, w0:w1], in_=values[:, 4 * w0 : 4 * w1]
+            )
+
+        def mask_times_t(g, c):
+            src = m_raw[g][:].rearrange("p r (s c) -> p r c s", c=2)
+            for r in range(4):
+                nc.scalar.activation(
+                    out=mt[g][c][:, r, :], in_=src[:, r, c, :], func=ACT.Copy, scale=t_sb[:, r : r + 1]
+                )
+
+        def sigmoid(a, g, first=0):
+            flat = "p h x -> p (h x)"
+            nc.scalar.activation(
+                out=gate[a][g][:].rearrange(flat)[:, first:],
+                in_=og_raw[a][g][:].rearrange(flat)[:, first:],
+                func=ACT.Sigmoid,
+            )
+
+        def scores(u):
+            a, g, c = unit(u)
+            for r in range(4):
+                for hh in range(2):
+                    rows = slice(ROWS * hh, ROWS * (hh + 1))
+                    tokens = slice(P * r, P * (r + 1))
+                    queries = slice(P * c, P * (c + 1))
+                    nc.tensor.matmul_mx(
+                        out=score_banks[hh][u % 3][:, r, :],
+                        lhsT=k_mx[a][1][rows, tokens].bitcast(FP8X4),
+                        lhsT_scale=k_mx[a][2][rows, tokens],
+                        rhs=q_mx[a][g][1][rows, queries].bitcast(FP8X4),
+                        rhs_scale=q_mx[a][g][2][rows, queries],
+                        start=True,
+                        stop=True,
+                    )
+
+        def weights(u, hh):
+            a, g, c = unit(u)
+            dst = w_mx[u][0][:, 512 * hh : 512 * (hh + 1)].rearrange("p (s i r) -> p s r i", i=2, r=4)
+            nc.vector.tensor_tensor(
+                out=dst,
+                in0=score_banks[hh][u % 3][:].rearrange("p r (s i) -> p s r i", i=2),
+                in1=mt[g][c][:].rearrange("p r (s i) -> p s r i", i=2),
+                op=MULT,
+            )
+
+        def values_product(u, hh):
+            a, g, c = unit(u)
+            cols = slice(P * hh, P * (hh + 1))
+            nc.tensor.matmul_mx(
+                out=y_banks[u % 2][:, hh, :],
+                lhsT=w_mx[u][1][:, cols].bitcast(FP8X4),
+                lhsT_scale=w_mx[u][2][:, cols],
+                rhs=v_mx[a][1][:, cols].bitcast(FP8X4),
+                rhs_scale=v_mx[a][2][:, cols],
+                start=True,
+                stop=True,
+            )
+
+        def gated(u):
+            a, g, c = unit(u)
+            cols = slice(E * c, E * (c + 1))
+            nc.vector.scalar_tensor_tensor(
+                out=res[a][g][:, :, cols],
+                in0=y_banks[u % 2][:, 0:2, :],
+                scalar=1.0 / 16.0,
+                in1=gate[a][g][:, :, cols],
+                op0=MULT,
+                op1=MULT,
+            )
+
+        def both_products(u):
+            values_product(u, 0)
+            values_product(u, 1)
+
+        def store(a, g, cols=slice(0, 2 * E)):
+            nc.sync.dma_start(out=rows_of(out, a, g)[:, :, cols], in_=res[a][g][:, :, cols])
+
+        nc.scalar.dma_start(out=t_sb[:], in_=t.rearrange("(p r) o -> p (r o)", r=4))
+        load_k(0, 0)
+        nc.scalar.dma_start(out=og_first[:], in_=rows_of(og, 0, 0)[:, 0, 0:EARLY])
+        nc.scalar.activation(out=gate[0][0][:, 0, 0:EARLY], in_=og_first[:], func=ACT.Sigmoid)
+        load_q(0, 0)
+        load_mask(0)
+        load_q(0, 1)
+        load_mask(1)
+        load_q(1, 0)
+        load_k(1, 0)
+        load_k(1, 1)
+        load_v(0)
+        load_og(0, 0)
+        load_q(1, 1)
+        load_og(0, 1)
+        load_v(1)
+        load_og(1, 0)
+        load_og(1, 1)
+
+        cast_k("vector", 0, 0, 0, K_SPLIT)
+        cast_k("scalar", 0, 0, K_SPLIT, P)
+        cast_q("scalar", 0, 0, 0, Q_SPLIT)
+        quantize(k_mx[0])
+        cast_q("vector", 0, 0, Q_SPLIT, P)
+        quantize(q_mx[0][0])
+        mask_times_t(0, 0)
+        mask_times_t(0, 1)
+        cast_q("scalar", 0, 1, 0, P)
+        mask_times_t(1, 0)
+        mask_times_t(1, 1)
+        cast_q("scalar", 1, 0, 0, P)
+        cast_k("scalar", 1, 0, 0, P // 2)
+        cast_k("scalar", 1, 1, 0, P // 2)
+        cast_v(0)
+        sigmoid(0, 0, EARLY)
+        cast_q("scalar", 1, 1, 0, P)
+        sigmoid(0, 1)
+        cast_v(1)
+        sigmoid(1, 0)
+        sigmoid(1, 1)
+
+        scores(0)
+        scores(1)
+        weights(0, 0)
+        weights(0, 1)
+        weights(1, 0)
+        quantize(q_mx[0][1])
+        scores(2)
+        scores(3)
+        quantize(w_mx[0])
+        weights(1, 1)
+        weights(2, 0)
+        quantize(w_mx[1])
+        weights(2, 1)
+        quantize(q_mx[1][0])
+        weights(3, 0)
+        quantize(w_mx[2])
+        weights(3, 1)
+        quantize(k_mx[1])
+        scores(4)
+        scores(5)
+        quantize(w_mx[3])
+        weights(4, 0)
+        quantize(v_mx[0])
+        both_products(0)
+        both_products(1)
+        weights(4, 1)
+        weights(5, 0)
+        quantize(w_mx[4])
+        gated(0)
+        gated(1)
+        both_products(2)
+        both_products(3)
+        store(0, 0)
+        quantize(q_mx[1][1])
+        scores(6)
+        scores(7)
+        weights(5, 1)
+        gated(2)
+        gated(3)
+        store(0, 1)
+        weights(6, 0)
+        quantize(w_mx[5])
+        quantize(v_mx[1])
+        both_products(4)
+        both_products(5)
+        weights(6, 1)
+        weights(7, 0)
+        quantize(w_mx[6])
+        gated(4)
+        both_products(6)
+        gated(5)
+        store(1, 0)
+        weights(7, 1)
+        quantize(w_mx[7], 0, P)
+        values_product(7, 0)
+        gated(6)
+        store(1, 1, slice(0, E))
+        quantize(w_mx[7], P, 2 * P)
+        values_product(7, 1)
+        gated(7)
+        store(1, 1, slice(E, 2 * E))

@@ -15,10 +15,9 @@ ACT = mybir.ActivationFunctionType
 
 P = 128
 ROWS = 64
-HALF = 256
-K_SPLIT = 84
-Q_SPLIT = 80
+SPLIT = 84
 EARLY = 8
+NASIDE = 0
 
 
 def tile_rows_a_lin_mask_gate_kernel(tc, qT, kT, t, v, mask, og, out):
@@ -41,253 +40,221 @@ def tile_rows_a_lin_mask_gate_kernel(tc, qT, kT, t, v, mask, og, out):
                 tile(name + "_scales", [P, words], U8),
             )
 
-        score_banks = [[ps.tile([P, 4, P], F32, name="score%d_%d" % (hh, i)) for i in range(3)] for hh in range(2)]
-        y_banks = [ps.tile([P, 4, E], F32, name="y%d" % i) for i in range(2)]
+        score_banks = [[ps.tile([P, 4, P], F32, name="score%d_%d" % (g, i)) for i in range(3)] for g in range(2)]
+        y_banks = [ps.tile([P, 4 * E], F32, name="y%d" % i) for i in range(2)]
 
         t_sb = tile("t_sb", [P, 4], F32)
         og_first = tile("og_first", [P, EARLY], F32)
-        k_raw = [[tile("k_raw0", [P, 4, N], F32)], [tile("k_raw1_%d" % i, [P, 4, HALF], F32) for i in range(2)]]
-        q_raw = [[tile("q_raw%d%d" % (a, g), [P, 4, HALF], F32) for g in range(2)] for a in range(2)]
-        m_raw = [tile("m_raw%d" % g, [P, 4, HALF], F32) for g in range(2)]
+        k_raw = [tile("k_raw%d" % a, [P, 4, N], F32) for a in range(2)]
+        q_raw = [tile("q_raw%d" % a, [P, 4, NQ], F32) for a in range(2)]
+        m_raw = tile("m_raw", [P, 4, NQ], F32)
         v_raw = [tile("v_raw%d" % a, [P, 2, 4 * E], F32) for a in range(2)]
-        og_raw = [[tile("og_raw%d%d" % (a, g), [P, 2, 2 * E], F32) for g in range(2)] for a in range(2)]
-        gate = [[tile("gate%d%d" % (a, g), [P, 2, 2 * E], F32) for g in range(2)] for a in range(2)]
-        res = [[tile("res%d%d" % (a, g), [P, 2, 2 * E], F32) for g in range(2)] for a in range(2)]
-        mt = [[tile("mt%d%d" % (g, c), [P, 4, P], F32) for c in range(2)] for g in range(2)]
+        og_raw = [tile("og_raw%d" % h, [P, 4 * E], F32) for h in range(H)]
+        gate = [tile("gate%d" % h, [P, 4 * E], F32) for h in range(H)]
+        res = [tile("res%d" % h, [P, 4 * E], F32) for h in range(H)]
+        y_sb = [tile("y_sb%d" % h, [P, 4 * E], F32) for h in range(NASIDE)]
+        mt = [tile("mt%d" % cc, [P, 2, 4, P], F32) for cc in range(2)]
         k_mx = [mx_tiles("k%d" % a, N) for a in range(2)]
-        q_mx = [[mx_tiles("q%d%d" % (a, g), HALF) for g in range(2)] for a in range(2)]
+        q_mx = [mx_tiles("q%d" % a, NQ) for a in range(2)]
         v_mx = [mx_tiles("v%d" % a, 2 * E) for a in range(2)]
-        w_mx = [mx_tiles("w%d" % u, 2 * P) for u in range(8)]
+        w_mx = [mx_tiles("w%d" % h, NQ) for h in range(H)]
 
-        def unit(u):
-            return u // 4, (u // 2) % 2, u % 2
-
-        def load_k(a, i):
-            raw = k_raw[a][i]
-            width = raw.shape[2]
-            src = k_rows[512 * a : 512 * (a + 1), width * i : width * (i + 1)]
-            nc.sync.dma_start(out=raw[:], in_=src.rearrange("(p j) w -> p j w", j=4))
-
-        def load_q(a, g):
-            src = q_rows[512 * a : 512 * (a + 1), HALF * g : HALF * (g + 1)]
-            nc.sync.dma_start(out=q_raw[a][g][:], in_=src.rearrange("(p j) w -> p j w", j=4))
-
-        def load_mask(g):
-            src = mask[:, HALF * g : HALF * (g + 1)]
-            nc.sync.dma_start(out=m_raw[g][:], in_=src.rearrange("(p r) w -> p r w", r=4))
+        def load_features(raw, rows, a):
+            nc.sync.dma_start(out=raw[a][:], in_=rows[512 * a : 512 * (a + 1), :].rearrange("(p j) w -> p j w", j=4))
 
         def load_v(a):
             nc.sync.dma_start(out=v_raw[a][:], in_=v[2 * a : 2 * a + 2].rearrange("h (p r) e -> p h (r e)", r=4))
 
-        def rows_of(x, a, g):
-            return x[2 * a : 2 * a + 2, HALF * g : HALF * (g + 1), :].rearrange("h (p c) e -> p h (c e)", c=2)
+        def rows_of(x, h):
+            return x[h].rearrange("(p c) e -> p (c e)", c=4)
 
-        def load_og(a, g):
-            nc.sync.dma_start(out=og_raw[a][g][:], in_=rows_of(og, a, g))
+        def load_og(h):
+            nc.sync.dma_start(out=og_raw[h][:], in_=rows_of(og, h))
 
-        def copy_on(eng, dst, src):
-            if eng == "vector":
-                nc.vector.tensor_copy(out=dst, in_=src)
-            else:
-                nc.scalar.copy(out=dst, in_=src)
-
-        def cast_k(eng, a, i, s0, s1):
-            raw = k_raw[a][i]
-            base = i * raw.shape[2] // 4
-            dst = k_mx[a][0][:].rearrange("p (rr rl s j) -> p rr s j rl", rr=2, rl=2, j=4)
-            src = raw[:].rearrange("p j (s rr rl) -> p rr s j rl", rr=2, rl=2)
-            copy_on(eng, dst[:, :, base + s0 : base + s1], src[:, :, s0:s1])
-
-        def cast_q(eng, a, g, s0, s1):
-            dst = q_mx[a][g][0][:].rearrange("p (c s j) -> p s j c", c=2, j=4)
-            src = q_raw[a][g][:].rearrange("p j (s c) -> p s j c", c=2)
-            copy_on(eng, dst[:, s0:s1], src[:, s0:s1])
+        def deal(copy, raw, mx, halves, s0, s1):
+            dst = mx[0][:].rearrange("p (cc cl s j) -> p cc s j cl", cc=2, cl=2, j=4)
+            src = raw[:].rearrange("p j (s cc cl) -> p cc s j cl", cc=2, cl=2)
+            copy(out=dst[:, halves, s0:s1], in_=src[:, halves, s0:s1])
 
         def cast_v(a):
             dst = v_mx[a][0][:].rearrange("p (h e i r) -> p h e r i", h=2, i=2, r=4)
             src = v_raw[a][:].rearrange("p h (r e i) -> p h e r i", r=4, i=2)
             nc.scalar.copy(out=dst, in_=src)
 
-        def quantize(mx, w0=0, w1=None):
+        def quantize(mx, w0, w1):
             values, codes, scales = mx
-            w1 = codes.shape[1] if w1 is None else w1
             nc.vector.quantize_mx(
                 out=codes[:, w0:w1].bitcast(FP8X4), scales=scales[:, w0:w1], in_=values[:, 4 * w0 : 4 * w1]
             )
 
-        def mask_times_t(g, c):
-            src = m_raw[g][:].rearrange("p r (s c) -> p r c s", c=2)
-            for r in range(4):
-                nc.scalar.activation(
-                    out=mt[g][c][:, r, :], in_=src[:, r, c, :], func=ACT.Copy, scale=t_sb[:, r : r + 1]
-                )
+        def mask_views(cc, r):
+            dst = mt[cc][:].rearrange("p cl r s -> p r s cl")[:, r]
+            src = m_raw[:].rearrange("p r (s cc cl) -> p r cc s cl", cc=2, cl=2)[:, r, cc]
+            return dst, src
 
-        def sigmoid(a, g, first=0):
-            flat = "p h x -> p (h x)"
-            nc.scalar.activation(
-                out=gate[a][g][:].rearrange(flat)[:, first:],
-                in_=og_raw[a][g][:].rearrange(flat)[:, first:],
-                func=ACT.Sigmoid,
-            )
+        def mask_times_t_scalar(cc, r):
+            dst, src = mask_views(cc, r)
+            nc.scalar.activation(out=dst, in_=src, func=ACT.Copy, scale=t_sb[:, r : r + 1])
 
-        def scores(u):
-            a, g, c = unit(u)
-            for r in range(4):
-                for hh in range(2):
-                    rows = slice(ROWS * hh, ROWS * (hh + 1))
-                    tokens = slice(P * r, P * (r + 1))
-                    queries = slice(P * c, P * (c + 1))
-                    nc.tensor.matmul_mx(
-                        out=score_banks[hh][u % 3][:, r, :],
-                        lhsT=k_mx[a][1][rows, tokens].bitcast(FP8X4),
-                        lhsT_scale=k_mx[a][2][rows, tokens],
-                        rhs=q_mx[a][g][1][rows, queries].bitcast(FP8X4),
-                        rhs_scale=q_mx[a][g][2][rows, queries],
-                        start=True,
-                        stop=True,
-                    )
+        def mask_times_t_vector(cc, r):
+            dst, src = mask_views(cc, r)
+            nc.vector.tensor_scalar(out=dst, in0=src, scalar1=t_sb[:, r : r + 1], scalar2=None, op0=MULT)
 
-        def weights(u, hh):
-            a, g, c = unit(u)
-            dst = w_mx[u][0][:, 512 * hh : 512 * (hh + 1)].rearrange("p (s i r) -> p s r i", i=2, r=4)
-            nc.vector.tensor_tensor(
-                out=dst,
-                in0=score_banks[hh][u % 3][:].rearrange("p r (s i) -> p s r i", i=2),
-                in1=mt[g][c][:].rearrange("p r (s i) -> p s r i", i=2),
-                op=MULT,
-            )
+        def sigmoid(h, first=0):
+            nc.scalar.activation(out=gate[h][:, first:], in_=og_raw[h][:, first:], func=ACT.Sigmoid)
 
-        def values_product(u, hh):
-            a, g, c = unit(u)
-            cols = slice(P * hh, P * (hh + 1))
+        def bank_of(h, c):
+            return score_banks[h % 2][(4 * (h // 2) + c) % 3]
+
+        def score_pass(h, c, r):
+            a, g = divmod(h, 2)
+            rows = slice(ROWS * g, ROWS * (g + 1))
+            tokens = slice(P * r, P * (r + 1))
+            queries = slice(P * c, P * (c + 1))
             nc.tensor.matmul_mx(
-                out=y_banks[u % 2][:, hh, :],
-                lhsT=w_mx[u][1][:, cols].bitcast(FP8X4),
-                lhsT_scale=w_mx[u][2][:, cols],
-                rhs=v_mx[a][1][:, cols].bitcast(FP8X4),
-                rhs_scale=v_mx[a][2][:, cols],
+                out=bank_of(h, c)[:, r, :],
+                lhsT=k_mx[a][1][rows, tokens].bitcast(FP8X4),
+                lhsT_scale=k_mx[a][2][rows, tokens],
+                rhs=q_mx[a][1][rows, queries].bitcast(FP8X4),
+                rhs_scale=q_mx[a][2][rows, queries],
                 start=True,
                 stop=True,
             )
 
-        def gated(u):
-            a, g, c = unit(u)
-            cols = slice(E * c, E * (c + 1))
-            nc.vector.scalar_tensor_tensor(
-                out=res[a][g][:, :, cols],
-                in0=y_banks[u % 2][:, 0:2, :],
-                scalar=1.0 / 16.0,
-                in1=gate[a][g][:, :, cols],
-                op0=MULT,
-                op1=MULT,
+        def scores(h, c):
+            for r in range(4):
+                score_pass(h, c, r)
+
+        def scores_side_by_side(first, second):
+            for r in range(4):
+                score_pass(first[0], first[1], r)
+                score_pass(second[0], second[1], r)
+
+        def weights(h, c):
+            dst = w_mx[h][0][:, 512 * c : 512 * (c + 1)].rearrange("p (s i r) -> p s r i", i=2, r=4)
+            nc.vector.tensor_tensor(
+                out=dst,
+                in0=bank_of(h, c)[:].rearrange("p r (s i) -> p s r i", i=2),
+                in1=mt[c // 2][:, c % 2].rearrange("p r (s i) -> p s r i", i=2),
+                op=MULT,
             )
 
-        def both_products(u):
-            values_product(u, 0)
-            values_product(u, 1)
+        def values_product(h, c0, c1, bank):
+            a, g = divmod(h, 2)
+            cols = slice(E * g, E * (g + 1))
+            for c in range(c0, c1):
+                words = slice(P * c, P * (c + 1))
+                nc.tensor.matmul_mx(
+                    out=y_banks[bank][:, E * c : E * (c + 1)],
+                    lhsT=w_mx[h][1][:, words].bitcast(FP8X4),
+                    lhsT_scale=w_mx[h][2][:, words],
+                    rhs=v_mx[a][1][:, cols].bitcast(FP8X4),
+                    rhs_scale=v_mx[a][2][:, cols],
+                    start=True,
+                    stop=True,
+                )
 
-        def store(a, g, cols=slice(0, 2 * E)):
-            nc.sync.dma_start(out=rows_of(out, a, g)[:, :, cols], in_=res[a][g][:, :, cols])
+        def gated(h, c0, c1, bank):
+            cols = slice(E * c0, E * c1)
+            nc.vector.scalar_tensor_tensor(
+                out=res[h][:, cols], in0=y_banks[bank][:, cols], scalar=1.0 / 16.0, in1=gate[h][:, cols], op0=MULT, op1=MULT
+            )
 
+        def gated_aside(h, bank):
+            nc.scalar.activation(out=y_sb[h][:], in_=y_banks[bank][:], func=ACT.Copy, scale=1.0 / 16.0)
+            for c in range(4):
+                cols = slice(E * c, E * (c + 1))
+                nc.gpsimd.tensor_tensor(out=res[h][:, cols], in0=y_sb[h][:, cols], in1=gate[h][:, cols], op=MULT)
+
+        def store(h, c0, c1):
+            cols = slice(E * c0, E * c1)
+            nc.sync.dma_start(out=rows_of(out, h)[:, cols], in_=res[h][:, cols])
+
+        both = slice(0, 2)
+        nc.scalar.dma_start(out=og_first[:], in_=rows_of(og, 0)[:, 0:EARLY])
         nc.scalar.dma_start(out=t_sb[:], in_=t.rearrange("(p r) o -> p (r o)", r=4))
-        load_k(0, 0)
-        nc.scalar.dma_start(out=og_first[:], in_=rows_of(og, 0, 0)[:, 0, 0:EARLY])
-        nc.scalar.activation(out=gate[0][0][:, 0, 0:EARLY], in_=og_first[:], func=ACT.Sigmoid)
-        load_q(0, 0)
-        load_mask(0)
-        load_q(0, 1)
-        load_mask(1)
-        load_q(1, 0)
-        load_k(1, 0)
-        load_k(1, 1)
+        nc.scalar.activation(out=gate[0][:, 0:EARLY], in_=og_first[:], func=ACT.Sigmoid)
+        load_features(k_raw, k_rows, 0)
+        load_features(q_raw, q_rows, 0)
+        nc.sync.dma_start(out=m_raw[:], in_=mask.rearrange("(p r) w -> p r w", r=4))
+        load_features(k_raw, k_rows, 1)
+        load_features(q_raw, q_rows, 1)
         load_v(0)
-        load_og(0, 0)
-        load_q(1, 1)
-        load_og(0, 1)
+        load_og(0)
+        load_og(1)
         load_v(1)
-        load_og(1, 0)
-        load_og(1, 1)
+        load_og(2)
+        load_og(3)
 
-        cast_k("vector", 0, 0, 0, K_SPLIT)
-        cast_k("scalar", 0, 0, K_SPLIT, P)
-        cast_q("scalar", 0, 0, 0, Q_SPLIT)
-        quantize(k_mx[0])
-        cast_q("vector", 0, 0, Q_SPLIT, P)
-        quantize(q_mx[0][0])
-        mask_times_t(0, 0)
-        mask_times_t(0, 1)
-        cast_q("scalar", 0, 1, 0, P)
-        mask_times_t(1, 0)
-        mask_times_t(1, 1)
-        cast_q("scalar", 1, 0, 0, P)
-        cast_k("scalar", 1, 0, 0, P // 2)
-        cast_k("scalar", 1, 1, 0, P // 2)
+        deal(nc.vector.tensor_copy, k_raw[0], k_mx[0], both, 0, SPLIT)
+        deal(nc.scalar.copy, k_raw[0], k_mx[0], both, SPLIT, P)
+        quantize(k_mx[0], 0, N)
+        deal(nc.vector.tensor_copy, q_raw[0], q_mx[0], both, 0, SPLIT)
+        deal(nc.scalar.copy, q_raw[0], q_mx[0], both, SPLIT, P)
+        quantize(q_mx[0], 0, NQ)
+        scores(0, 0)
+        scores(1, 0)
+        scores_side_by_side((0, 1), (1, 1))
+        scores_side_by_side((0, 2), (1, 2))
+        mask_times_t_scalar(0, 3)
+        for r in range(3):
+            mask_times_t_vector(0, r)
+        for r in range(4):
+            mask_times_t_scalar(1, r)
+        deal(nc.scalar.copy, k_raw[1], k_mx[1], both, 0, P)
+        deal(nc.scalar.copy, q_raw[1], q_mx[1], 0, 0, P)
+        deal(nc.scalar.copy, q_raw[1], q_mx[1], 1, 0, P)
         cast_v(0)
-        sigmoid(0, 0, EARLY)
-        cast_q("scalar", 1, 1, 0, P)
-        sigmoid(0, 1)
-        cast_v(1)
-        sigmoid(1, 0)
-        sigmoid(1, 1)
+        sigmoid(0, EARLY)
+        sigmoid(1)
 
-        scores(0)
-        scores(1)
         weights(0, 0)
-        weights(0, 1)
         weights(1, 0)
-        quantize(q_mx[0][1])
-        scores(2)
-        scores(3)
-        quantize(w_mx[0])
-        weights(1, 1)
+        scores_side_by_side((0, 3), (1, 3))
+        for c in range(1, 4):
+            weights(0, c)
+            weights(1, c)
+        quantize(k_mx[1], 0, N)
+        quantize(q_mx[1], 0, 2 * P)
+        scores(2, 0)
+        scores_side_by_side((2, 1), (3, 0))
+        quantize(w_mx[0], 0, NQ)
+        quantize(w_mx[1], 0, NQ)
+        quantize(q_mx[1], 2 * P, NQ)
+        scores_side_by_side((2, 2), (3, 1))
         weights(2, 0)
-        quantize(w_mx[1])
+        scores_side_by_side((2, 3), (3, 2))
         weights(2, 1)
-        quantize(q_mx[1][0])
+        quantize(v_mx[0], 0, 2 * E)
+        values_product(0, 0, 4, 0)
+        values_product(1, 0, 4, 1)
+        cast_v(1)
+        sigmoid(2)
+        sigmoid(3)
+        weights(2, 2)
+        gated(0, 0, 4, 0)
+        store(0, 0, 4)
+        weights(2, 3)
+        gated(1, 0, 4, 1)
+        store(1, 0, 4)
+        quantize(w_mx[2], 0, NQ)
+        quantize(v_mx[1], 0, 2 * E)
+        values_product(2, 0, 4, 0)
         weights(3, 0)
-        quantize(w_mx[2])
+        scores(3, 3)
         weights(3, 1)
-        quantize(k_mx[1])
-        scores(4)
-        scores(5)
-        quantize(w_mx[3])
-        weights(4, 0)
-        quantize(v_mx[0])
-        both_products(0)
-        both_products(1)
-        weights(4, 1)
-        weights(5, 0)
-        quantize(w_mx[4])
-        gated(0)
-        gated(1)
-        both_products(2)
-        both_products(3)
-        store(0, 0)
-        quantize(q_mx[1][1])
-        scores(6)
-        scores(7)
-        weights(5, 1)
-        gated(2)
-        gated(3)
-        store(0, 1)
-        weights(6, 0)
-        quantize(w_mx[5])
-        quantize(v_mx[1])
-        both_products(4)
-        both_products(5)
-        weights(6, 1)
-        weights(7, 0)
-        quantize(w_mx[6])
-        gated(4)
-        both_products(6)
-        gated(5)
-        store(1, 0)
-        weights(7, 1)
-        quantize(w_mx[7], 0, P)
-        values_product(7, 0)
-        gated(6)
-        store(1, 1, slice(0, E))
-        quantize(w_mx[7], P, 2 * P)
-        values_product(7, 1)
-        gated(7)
-        store(1, 1, slice(E, 2 * E))
+        gated(2, 0, 4, 0)
+        store(2, 0, 4)
+        quantize(w_mx[3], 0, 2 * P)
+        values_product(3, 0, 2, 1)
+        weights(3, 2)
+        weights(3, 3)
+        quantize(w_mx[3], 2 * P, 3 * P)
+        values_product(3, 2, 3, 0)
+        gated(3, 0, 2, 1)
+        store(3, 0, 2)
+        quantize(w_mx[3], 3 * P, NQ)
+        values_product(3, 3, 4, 1)
+        gated(3, 2, 3, 0)
+        gated(3, 3, 4, 1)
+        store(3, 2, 4)

@@ -17,7 +17,6 @@ P = 128
 ROWS = 64
 SPLIT = 84
 EARLY = 8
-NASIDE = 0
 
 
 def tile_rows_a_lin_mask_gate_kernel(tc, qT, kT, t, v, mask, og, out):
@@ -52,8 +51,8 @@ def tile_rows_a_lin_mask_gate_kernel(tc, qT, kT, t, v, mask, og, out):
         og_raw = [tile("og_raw%d" % h, [P, 4 * E], F32) for h in range(H)]
         gate = [tile("gate%d" % h, [P, 4 * E], F32) for h in range(H)]
         res = [tile("res%d" % h, [P, 4 * E], F32) for h in range(H)]
-        y_sb = [tile("y_sb%d" % h, [P, 4 * E], F32) for h in range(NASIDE)]
-        mt = [tile("mt%d" % cc, [P, 2, 4, P], F32) for cc in range(2)]
+        mt = [tile("mt%d" % cc, [P, 2, P, 4], F32) for cc in range(2)]
+        mt_rows = tile("mt_rows", [P, 4, P, 2], F32)
         k_mx = [mx_tiles("k%d" % a, N) for a in range(2)]
         q_mx = [mx_tiles("q%d" % a, NQ) for a in range(2)]
         v_mx = [mx_tiles("v%d" % a, 2 * E) for a in range(2)]
@@ -87,18 +86,24 @@ def tile_rows_a_lin_mask_gate_kernel(tc, qT, kT, t, v, mask, og, out):
                 out=codes[:, w0:w1].bitcast(FP8X4), scales=scales[:, w0:w1], in_=values[:, 4 * w0 : 4 * w1]
             )
 
-        def mask_views(cc, r):
-            dst = mt[cc][:].rearrange("p cl r s -> p r s cl")[:, r]
-            src = m_raw[:].rearrange("p r (s cc cl) -> p r cc s cl", cc=2, cl=2)[:, r, cc]
-            return dst, src
+        mask_pairs = m_raw[:].rearrange("p r (s cc cl) -> p cc s r cl", cc=2, cl=2)
 
-        def mask_times_t_scalar(cc, r):
-            dst, src = mask_views(cc, r)
-            nc.scalar.activation(out=dst, in_=src, func=ACT.Copy, scale=t_sb[:, r : r + 1])
+        def mask_times_t_vector(cc):
+            nc.vector.tensor_tensor(
+                out=mt[cc][:].rearrange("p cl s r -> p s r cl"),
+                in0=mask_pairs[:, cc],
+                in1=t_sb[:].unsqueeze(1).unsqueeze(3).to_broadcast([P, P, 4, 2]),
+                op=MULT,
+            )
 
-        def mask_times_t_vector(cc, r):
-            dst, src = mask_views(cc, r)
-            nc.vector.tensor_scalar(out=dst, in0=src, scalar1=t_sb[:, r : r + 1], scalar2=None, op0=MULT)
+        def mask_times_t_scalar(cc):
+            for r in range(4):
+                nc.scalar.activation(
+                    out=mt_rows[:, r], in_=mask_pairs[:, cc, :, r], func=ACT.Copy, scale=t_sb[:, r : r + 1]
+                )
+            nc.scalar.copy(
+                out=mt[cc][:].rearrange("p cl s r -> p s r cl"), in_=mt_rows[:].rearrange("p r s cl -> p s r cl")
+            )
 
         def sigmoid(h, first=0):
             nc.scalar.activation(out=gate[h][:, first:], in_=og_raw[h][:, first:], func=ACT.Sigmoid)
@@ -131,11 +136,11 @@ def tile_rows_a_lin_mask_gate_kernel(tc, qT, kT, t, v, mask, og, out):
                 score_pass(second[0], second[1], r)
 
         def weights(h, c):
-            dst = w_mx[h][0][:, 512 * c : 512 * (c + 1)].rearrange("p (s i r) -> p s r i", i=2, r=4)
+            dst = w_mx[h][0][:, 512 * c : 512 * (c + 1)].rearrange("p (s r) -> p s r", r=4)
             nc.vector.tensor_tensor(
                 out=dst,
-                in0=bank_of(h, c)[:].rearrange("p r (s i) -> p s r i", i=2),
-                in1=mt[c // 2][:, c % 2].rearrange("p r (s i) -> p s r i", i=2),
+                in0=bank_of(h, c)[:].rearrange("p r s -> p s r"),
+                in1=mt[c // 2][:, c % 2],
                 op=MULT,
             )
 
@@ -160,12 +165,6 @@ def tile_rows_a_lin_mask_gate_kernel(tc, qT, kT, t, v, mask, og, out):
                 out=res[h][:, cols], in0=y_banks[bank][:, cols], scalar=1.0 / 16.0, in1=gate[h][:, cols], op0=MULT, op1=MULT
             )
 
-        def gated_aside(h, bank):
-            nc.scalar.activation(out=y_sb[h][:], in_=y_banks[bank][:], func=ACT.Copy, scale=1.0 / 16.0)
-            for c in range(4):
-                cols = slice(E * c, E * (c + 1))
-                nc.gpsimd.tensor_tensor(out=res[h][:, cols], in0=y_sb[h][:, cols], in1=gate[h][:, cols], op=MULT)
-
         def store(h, c0, c1):
             cols = slice(E * c0, E * c1)
             nc.sync.dma_start(out=rows_of(out, h)[:, cols], in_=res[h][:, cols])
@@ -189,22 +188,20 @@ def tile_rows_a_lin_mask_gate_kernel(tc, qT, kT, t, v, mask, og, out):
         deal(nc.vector.tensor_copy, k_raw[0], k_mx[0], both, 0, SPLIT)
         deal(nc.scalar.copy, k_raw[0], k_mx[0], both, SPLIT, P)
         quantize(k_mx[0], 0, N)
-        deal(nc.vector.tensor_copy, q_raw[0], q_mx[0], both, 0, SPLIT)
-        deal(nc.scalar.copy, q_raw[0], q_mx[0], both, SPLIT, P)
-        quantize(q_mx[0], 0, NQ)
+        deal(nc.vector.tensor_copy, q_raw[0], q_mx[0], 0, 0, P)
+        deal(nc.scalar.copy, q_raw[0], q_mx[0], 1, 0, P)
+        quantize(q_mx[0], 0, 2 * P)
         scores(0, 0)
         scores(1, 0)
         scores_side_by_side((0, 1), (1, 1))
+        quantize(q_mx[0], 2 * P, NQ)
         scores_side_by_side((0, 2), (1, 2))
-        mask_times_t_scalar(0, 3)
-        for r in range(3):
-            mask_times_t_vector(0, r)
-        for r in range(4):
-            mask_times_t_scalar(1, r)
+        mask_times_t_vector(0)
+        mask_times_t_scalar(1)
         deal(nc.scalar.copy, k_raw[1], k_mx[1], both, 0, P)
         deal(nc.scalar.copy, q_raw[1], q_mx[1], 0, 0, P)
-        deal(nc.scalar.copy, q_raw[1], q_mx[1], 1, 0, P)
         cast_v(0)
+        deal(nc.scalar.copy, q_raw[1], q_mx[1], 1, 0, P)
         sigmoid(0, EARLY)
         sigmoid(1)
 
@@ -217,44 +214,44 @@ def tile_rows_a_lin_mask_gate_kernel(tc, qT, kT, t, v, mask, og, out):
         quantize(k_mx[1], 0, N)
         quantize(q_mx[1], 0, 2 * P)
         scores(2, 0)
-        scores_side_by_side((2, 1), (3, 0))
+        scores(3, 0)
+        scores_side_by_side((2, 1), (3, 1))
         quantize(w_mx[0], 0, NQ)
         quantize(w_mx[1], 0, NQ)
-        quantize(q_mx[1], 2 * P, NQ)
-        scores_side_by_side((2, 2), (3, 1))
-        weights(2, 0)
-        scores_side_by_side((2, 3), (3, 2))
-        weights(2, 1)
         quantize(v_mx[0], 0, 2 * E)
         values_product(0, 0, 4, 0)
+        weights(2, 0)
+        quantize(q_mx[1], 2 * P, NQ)
+        scores(2, 2)
         values_product(1, 0, 4, 1)
+        scores(2, 3)
+        scores(3, 2)
+        weights(3, 0)
+        scores(3, 3)
         cast_v(1)
         sigmoid(2)
         sigmoid(3)
-        weights(2, 2)
+        weights(2, 1)
         gated(0, 0, 4, 0)
         store(0, 0, 4)
-        weights(2, 3)
+        weights(3, 1)
         gated(1, 0, 4, 1)
         store(1, 0, 4)
-        quantize(w_mx[2], 0, NQ)
+        weights(2, 2)
+        weights(2, 3)
         quantize(v_mx[1], 0, 2 * E)
+        quantize(w_mx[2], 0, NQ)
         values_product(2, 0, 4, 0)
-        weights(3, 0)
-        scores(3, 3)
-        weights(3, 1)
-        gated(2, 0, 4, 0)
-        store(2, 0, 4)
+        weights(3, 2)
         quantize(w_mx[3], 0, 2 * P)
         values_product(3, 0, 2, 1)
-        weights(3, 2)
         weights(3, 3)
         quantize(w_mx[3], 2 * P, 3 * P)
-        values_product(3, 2, 3, 0)
+        quantize(w_mx[3], 3 * P, NQ)
+        values_product(3, 2, 4, 1)
+        gated(2, 0, 4, 0)
+        store(2, 0, 4)
         gated(3, 0, 2, 1)
         store(3, 0, 2)
-        quantize(w_mx[3], 3 * P, NQ)
-        values_product(3, 3, 4, 1)
-        gated(3, 2, 3, 0)
-        gated(3, 3, 4, 1)
+        gated(3, 2, 4, 1)
         store(3, 2, 4)

@@ -15,8 +15,9 @@ ACT = mybir.ActivationFunctionType
 
 P = 128
 ROWS = 64
-SPLIT = 84
+SPLIT = 88
 EARLY = 8
+RUN = (4, 4, 4, 2)
 
 
 def tile_rows_a_lin_mask_gate_kernel(tc, qT, kT, t, v, mask, og, out):
@@ -51,8 +52,8 @@ def tile_rows_a_lin_mask_gate_kernel(tc, qT, kT, t, v, mask, og, out):
         og_raw = [tile("og_raw%d" % h, [P, 4 * E], F32) for h in range(H)]
         gate = [tile("gate%d" % h, [P, 4 * E], F32) for h in range(H)]
         res = [tile("res%d" % h, [P, 4 * E], F32) for h in range(H)]
-        mt = [tile("mt%d" % cc, [P, 2, P, 4], F32) for cc in range(2)]
-        mt_rows = tile("mt_rows", [P, 4, P, 2], F32)
+        mt = [tile("mt%d" % half, [P, NQ // 2, 4], F32) for half in range(2)]
+        mt_rows = tile("mt_rows", [P, 4, NQ // 2], F32)
         k_mx = [mx_tiles("k%d" % a, N) for a in range(2)]
         q_mx = [mx_tiles("q%d" % a, NQ) for a in range(2)]
         v_mx = [mx_tiles("v%d" % a, 2 * E) for a in range(2)]
@@ -65,19 +66,31 @@ def tile_rows_a_lin_mask_gate_kernel(tc, qT, kT, t, v, mask, og, out):
             nc.sync.dma_start(out=v_raw[a][:], in_=v[2 * a : 2 * a + 2].rearrange("h (p r) e -> p h (r e)", r=4))
 
         def rows_of(x, h):
-            return x[h].rearrange("(p c) e -> p (c e)", c=4)
+            return x[h].rearrange("(g p c) e -> p g (c e)", p=P, c=RUN[h])
 
         def load_og(h):
-            nc.sync.dma_start(out=og_raw[h][:], in_=rows_of(og, h))
+            rows = rows_of(og, h)
+            nc.sync.dma_start(out=og_raw[h][:].rearrange("p (g x) -> p g x", g=rows.shape[1]), in_=rows)
 
-        def deal(copy, raw, mx, halves, s0, s1):
-            dst = mx[0][:].rearrange("p (cc cl s j) -> p cc s j cl", cc=2, cl=2, j=4)
-            src = raw[:].rearrange("p j (s cc cl) -> p cc s j cl", cc=2, cl=2)
-            copy(out=dst[:, halves, s0:s1], in_=src[:, halves, s0:s1])
+        def round_k_vector(a, s0, s1):
+            dst = k_mx[a][0][:].rearrange("p (rr rl s j) -> p rr s j rl", rr=2, rl=2, j=4)
+            src = k_raw[a][:].rearrange("p j (s rr rl) -> p rr s j rl", rr=2, rl=2)
+            nc.vector.tensor_copy(out=dst[:, :, s0:s1], in_=src[:, :, s0:s1])
+
+        def round_k_scalar(a, s0, s1):
+            dst = k_mx[a][0][:].rearrange("p (r s j) -> p s j r", r=4, j=4)
+            src = k_raw[a][:].rearrange("p j (s r) -> p s j r", r=4)
+            nc.scalar.copy(out=dst[:, s0:s1], in_=src[:, s0:s1])
+
+        def round_q(copy, run, a, half):
+            cols = slice(NQ // 2 * half, NQ // 2 * (half + 1))
+            dst = q_mx[a][0][:].rearrange("p (w j) -> p w j", j=4)[:, cols].rearrange("p (n i) j -> p n j i", i=run)
+            src = q_raw[a][:, :, cols].rearrange("p j (n i) -> p n j i", i=run)
+            copy(out=dst, in_=src)
 
         def cast_v(a):
-            dst = v_mx[a][0][:].rearrange("p (h e i r) -> p h e r i", h=2, i=2, r=4)
-            src = v_raw[a][:].rearrange("p h (r e i) -> p h e r i", r=4, i=2)
+            dst = v_mx[a][0][:].rearrange("p (h n i r) -> p h n r i", h=2, i=4, r=4)
+            src = v_raw[a][:].rearrange("p h (r n i) -> p h n r i", r=4, i=4)
             nc.scalar.copy(out=dst, in_=src)
 
         def quantize(mx, w0, w1):
@@ -86,23 +99,25 @@ def tile_rows_a_lin_mask_gate_kernel(tc, qT, kT, t, v, mask, og, out):
                 out=codes[:, w0:w1].bitcast(FP8X4), scales=scales[:, w0:w1], in_=values[:, 4 * w0 : 4 * w1]
             )
 
-        mask_pairs = m_raw[:].rearrange("p r (s cc cl) -> p cc s r cl", cc=2, cl=2)
-
-        def mask_times_t_vector(cc):
+        def mask_times_t_vector(half):
+            cols = slice(NQ // 2 * half, NQ // 2 * (half + 1))
             nc.vector.tensor_tensor(
-                out=mt[cc][:].rearrange("p cl s r -> p s r cl"),
-                in0=mask_pairs[:, cc],
-                in1=t_sb[:].unsqueeze(1).unsqueeze(3).to_broadcast([P, P, 4, 2]),
+                out=mt[half][:].rearrange("p (n i) r -> p n r i", i=2),
+                in0=m_raw[:, :, cols].rearrange("p r (n i) -> p n r i", i=2),
+                in1=t_sb[:].unsqueeze(1).unsqueeze(3).to_broadcast([P, NQ // 4, 4, 2]),
                 op=MULT,
             )
 
-        def mask_times_t_scalar(cc):
+        def scale_mask_row(half, r):
+            cols = slice(NQ // 2 * half, NQ // 2 * (half + 1))
+            nc.scalar.activation(out=mt_rows[:, r], in_=m_raw[:, r, cols], func=ACT.Copy, scale=t_sb[:, r : r + 1])
+
+        def mask_times_t_scalar(half):
             for r in range(4):
-                nc.scalar.activation(
-                    out=mt_rows[:, r], in_=mask_pairs[:, cc, :, r], func=ACT.Copy, scale=t_sb[:, r : r + 1]
-                )
+                scale_mask_row(half, r)
             nc.scalar.copy(
-                out=mt[cc][:].rearrange("p cl s r -> p s r cl"), in_=mt_rows[:].rearrange("p r s cl -> p s r cl")
+                out=mt[half][:].rearrange("p (n i) r -> p n r i", i=4),
+                in_=mt_rows[:].rearrange("p r (n i) -> p n r i", i=4),
             )
 
         def sigmoid(h, first=0):
@@ -136,11 +151,15 @@ def tile_rows_a_lin_mask_gate_kernel(tc, qT, kT, t, v, mask, og, out):
                 score_pass(second[0], second[1], r)
 
         def weights(h, c):
-            dst = w_mx[h][0][:, 512 * c : 512 * (c + 1)].rearrange("p (s r) -> p s r", r=4)
+            run = RUN[h]
+            count = P // run
+            group, place = divmod(c, run)
+            dst = w_mx[h][0][:].rearrange("p (g x s r) -> p g x s r", x=run, s=P, r=4)
+            queries = slice(P * (c % 2), P * (c % 2 + 1))
             nc.vector.tensor_tensor(
-                out=dst,
-                in0=bank_of(h, c)[:].rearrange("p r s -> p s r"),
-                in1=mt[c // 2][:, c % 2],
+                out=dst[:, group, :, count * place : count * (place + 1)],
+                in0=bank_of(h, c)[:].rearrange("p r (s x) -> p x s r", x=run),
+                in1=mt[c // 2][:, queries].rearrange("p (s x) r -> p x s r", x=run),
                 op=MULT,
             )
 
@@ -165,17 +184,17 @@ def tile_rows_a_lin_mask_gate_kernel(tc, qT, kT, t, v, mask, og, out):
                 out=res[h][:, cols], in0=y_banks[bank][:, cols], scalar=1.0 / 16.0, in1=gate[h][:, cols], op0=MULT, op1=MULT
             )
 
-        def store(h, c0, c1):
-            cols = slice(E * c0, E * c1)
-            nc.sync.dma_start(out=rows_of(out, h)[:, cols], in_=res[h][:, cols])
+        def store(h, group):
+            width = RUN[h] * E
+            nc.sync.dma_start(out=rows_of(out, h)[:, group], in_=res[h][:, width * group : width * (group + 1)])
 
-        both = slice(0, 2)
-        nc.scalar.dma_start(out=og_first[:], in_=rows_of(og, 0)[:, 0:EARLY])
+        nc.scalar.dma_start(out=og_first[:], in_=rows_of(og, 0)[:, 0, 0:EARLY])
         nc.scalar.dma_start(out=t_sb[:], in_=t.rearrange("(p r) o -> p (r o)", r=4))
         nc.scalar.activation(out=gate[0][:, 0:EARLY], in_=og_first[:], func=ACT.Sigmoid)
         load_features(k_raw, k_rows, 0)
         load_features(q_raw, q_rows, 0)
-        nc.sync.dma_start(out=m_raw[:], in_=mask.rearrange("(p r) w -> p r w", r=4))
+        for r0 in (0, 2):
+            nc.sync.dma_start(out=m_raw[:, r0 : r0 + 2], in_=mask.rearrange("(p r) w -> p r w", r=4)[:, r0 : r0 + 2])
         load_features(k_raw, k_rows, 1)
         load_features(q_raw, q_rows, 1)
         load_v(0)
@@ -185,11 +204,11 @@ def tile_rows_a_lin_mask_gate_kernel(tc, qT, kT, t, v, mask, og, out):
         load_og(2)
         load_og(3)
 
-        deal(nc.vector.tensor_copy, k_raw[0], k_mx[0], both, 0, SPLIT)
-        deal(nc.scalar.copy, k_raw[0], k_mx[0], both, SPLIT, P)
+        round_k_vector(0, 0, SPLIT)
+        round_k_scalar(0, SPLIT, P)
         quantize(k_mx[0], 0, N)
-        deal(nc.vector.tensor_copy, q_raw[0], q_mx[0], 0, 0, P)
-        deal(nc.scalar.copy, q_raw[0], q_mx[0], 1, 0, P)
+        round_q(nc.vector.tensor_copy, 2, 0, 0)
+        round_q(nc.scalar.copy, 4, 0, 1)
         quantize(q_mx[0], 0, 2 * P)
         scores(0, 0)
         scores(1, 0)
@@ -198,10 +217,10 @@ def tile_rows_a_lin_mask_gate_kernel(tc, qT, kT, t, v, mask, og, out):
         scores_side_by_side((0, 2), (1, 2))
         mask_times_t_vector(0)
         mask_times_t_scalar(1)
-        deal(nc.scalar.copy, k_raw[1], k_mx[1], both, 0, P)
-        deal(nc.scalar.copy, q_raw[1], q_mx[1], 0, 0, P)
+        round_k_scalar(1, 0, P)
+        round_q(nc.scalar.copy, 4, 1, 0)
         cast_v(0)
-        deal(nc.scalar.copy, q_raw[1], q_mx[1], 1, 0, P)
+        round_q(nc.scalar.copy, 4, 1, 1)
         sigmoid(0, EARLY)
         sigmoid(1)
 
@@ -212,46 +231,44 @@ def tile_rows_a_lin_mask_gate_kernel(tc, qT, kT, t, v, mask, og, out):
             weights(0, c)
             weights(1, c)
         quantize(k_mx[1], 0, N)
+        quantize(w_mx[0], 0, 2 * P)
         quantize(q_mx[1], 0, 2 * P)
         scores(2, 0)
         scores(3, 0)
         scores_side_by_side((2, 1), (3, 1))
-        quantize(w_mx[0], 0, NQ)
+        quantize(w_mx[0], 2 * P, NQ)
         quantize(w_mx[1], 0, NQ)
+        weights(2, 0)
         quantize(v_mx[0], 0, 2 * E)
         values_product(0, 0, 4, 0)
-        weights(2, 0)
-        quantize(q_mx[1], 2 * P, NQ)
-        scores(2, 2)
         values_product(1, 0, 4, 1)
-        scores(2, 3)
-        scores(3, 2)
         weights(3, 0)
-        scores(3, 3)
+        quantize(q_mx[1], 2 * P, NQ)
+        scores_side_by_side((2, 2), (3, 2))
+        scores_side_by_side((2, 3), (3, 3))
         cast_v(1)
         sigmoid(2)
         sigmoid(3)
         weights(2, 1)
         gated(0, 0, 4, 0)
-        store(0, 0, 4)
+        store(0, 0)
         weights(3, 1)
         gated(1, 0, 4, 1)
-        store(1, 0, 4)
+        store(1, 0)
         weights(2, 2)
+        quantize(w_mx[3], 0, 2 * P)
         weights(2, 3)
         quantize(v_mx[1], 0, 2 * E)
+        values_product(3, 0, 2, 1)
         quantize(w_mx[2], 0, NQ)
         values_product(2, 0, 4, 0)
         weights(3, 2)
-        quantize(w_mx[3], 0, 2 * P)
-        values_product(3, 0, 2, 1)
+        gated(3, 0, 2, 1)
+        store(3, 0)
         weights(3, 3)
-        quantize(w_mx[3], 2 * P, 3 * P)
-        quantize(w_mx[3], 3 * P, NQ)
+        quantize(w_mx[3], 2 * P, NQ)
         values_product(3, 2, 4, 1)
         gated(2, 0, 4, 0)
-        store(2, 0, 4)
-        gated(3, 0, 2, 1)
-        store(3, 0, 2)
+        store(2, 0)
         gated(3, 2, 4, 1)
-        store(3, 2, 4)
+        store(3, 1)

from contextlib import ExitStack

import concourse.mybir as mybir

H, D, NQ, N, E = 4, 256, 512, 512, 128
FLOPS = 2 * H * N * NQ * D + 2 * H * N * NQ * E

F32 = mybir.dt.float32
BF16 = mybir.dt.bfloat16
U32 = mybir.dt.uint32
U8 = mybir.dt.uint8
FP8X4 = mybir.dt.float8_e4m3fn_x4
MULT = mybir.AluOpType.mult
ACT = mybir.ActivationFunctionType

P = 128
ROWS = 64
SPLIT = 88
EARLY = 8
RUN = (4, 4, 4, 2)


def tile_rows_a_lin_mask_gate_kernel(tc, qT, kT, t, v, mask, og, out):
    nc = tc.nc
    q_rows = qT.rearrange("h d w -> (h d) w")
    k_rows = kT.rearrange("h d w -> (h d) w")

    with ExitStack() as ctx:
        sb = ctx.enter_context(tc.tile_pool(name="sb", bufs=1))
        ps = ctx.enter_context(tc.psum_pool(name="ps", bufs=1))
        ctx.enter_context(tc.manual_schedule())

        def tile(name, shape, dtype):
            return sb.tile(shape, dtype, name=name, align_bytes=64)

        def mx_tiles(name, words):
            return (
                tile(name + "_bf", [P, words * 4], BF16),
                tile(name + "_codes", [P, words], U32),
                tile(name + "_scales", [P, words], U8),
            )

        score_banks = [[ps.tile([P, 4, P], F32, name="score%d_%d" % (g, i)) for i in range(3)] for g in range(2)]
        y_banks = [ps.tile([P, 4 * E], F32, name="y%d" % i) for i in range(2)]

        t_sb = tile("t_sb", [P, 4], F32)
        og_first = tile("og_first", [P, EARLY], F32)
        k_raw = [tile("k_raw%d" % a, [P, 4, N], F32) for a in range(2)]
        q_raw = [tile("q_raw%d" % a, [P, 4, NQ], F32) for a in range(2)]
        m_raw = tile("m_raw", [P, 4, NQ], F32)
        v_raw = [tile("v_raw%d" % a, [P, 2, 4 * E], F32) for a in range(2)]
        og_raw = [tile("og_raw%d" % h, [P, 4 * E], F32) for h in range(H)]
        gate = [tile("gate%d" % h, [P, 4 * E], F32) for h in range(H)]
        res = [tile("res%d" % h, [P, 4 * E], F32) for h in range(H)]
        mt = [tile("mt%d" % half, [P, NQ // 2, 4], F32) for half in range(2)]
        mt_rows = tile("mt_rows", [P, 4, NQ // 2], F32)
        k_mx = [mx_tiles("k%d" % a, N) for a in range(2)]
        q_mx = [mx_tiles("q%d" % a, NQ) for a in range(2)]
        v_mx = [mx_tiles("v%d" % a, 2 * E) for a in range(2)]
        w_mx = [mx_tiles("w%d" % h, NQ) for h in range(H)]

        def load_features(raw, rows, a):
            nc.sync.dma_start(out=raw[a][:], in_=rows[512 * a : 512 * (a + 1), :].rearrange("(p j) w -> p j w", j=4))

        def load_v(a):
            nc.sync.dma_start(out=v_raw[a][:], in_=v[2 * a : 2 * a + 2].rearrange("h (p r) e -> p h (r e)", r=4))

        def rows_of(x, h):
            return x[h].rearrange("(g p c) e -> p g (c e)", p=P, c=RUN[h])

        def load_og(h):
            rows = rows_of(og, h)
            nc.sync.dma_start(out=og_raw[h][:].rearrange("p (g x) -> p g x", g=rows.shape[1]), in_=rows)

        def round_k_vector(a, s0, s1):
            dst = k_mx[a][0][:].rearrange("p (rr rl s j) -> p rr s j rl", rr=2, rl=2, j=4)
            src = k_raw[a][:].rearrange("p j (s rr rl) -> p rr s j rl", rr=2, rl=2)
            nc.vector.tensor_copy(out=dst[:, :, s0:s1], in_=src[:, :, s0:s1])

        def round_k_scalar(a, s0, s1):
            dst = k_mx[a][0][:].rearrange("p (r s j) -> p s j r", r=4, j=4)
            src = k_raw[a][:].rearrange("p j (s r) -> p s j r", r=4)
            nc.scalar.copy(out=dst[:, s0:s1], in_=src[:, s0:s1])

        def round_q(copy, run, a, half):
            cols = slice(NQ // 2 * half, NQ // 2 * (half + 1))
            dst = q_mx[a][0][:].rearrange("p (w j) -> p w j", j=4)[:, cols].rearrange("p (n i) j -> p n j i", i=run)
            src = q_raw[a][:, :, cols].rearrange("p j (n i) -> p n j i", i=run)
            copy(out=dst, in_=src)

        def cast_v(a):
            dst = v_mx[a][0][:].rearrange("p (h n i r) -> p h n r i", h=2, i=4, r=4)
            src = v_raw[a][:].rearrange("p h (r n i) -> p h n r i", r=4, i=4)
            nc.scalar.copy(out=dst, in_=src)

        def quantize(mx, w0, w1):
            values, codes, scales = mx
            nc.vector.quantize_mx(
                out=codes[:, w0:w1].bitcast(FP8X4), scales=scales[:, w0:w1], in_=values[:, 4 * w0 : 4 * w1]
            )

        def mask_times_t_vector(half):
            cols = slice(NQ // 2 * half, NQ // 2 * (half + 1))
            nc.vector.tensor_tensor(
                out=mt[half][:].rearrange("p (n i) r -> p n r i", i=2),
                in0=m_raw[:, :, cols].rearrange("p r (n i) -> p n r i", i=2),
                in1=t_sb[:].unsqueeze(1).unsqueeze(3).to_broadcast([P, NQ // 4, 4, 2]),
                op=MULT,
            )

        def scale_mask_row(half, r):
            cols = slice(NQ // 2 * half, NQ // 2 * (half + 1))
            nc.scalar.activation(out=mt_rows[:, r], in_=m_raw[:, r, cols], func=ACT.Copy, scale=t_sb[:, r : r + 1])

        def mask_times_t_scalar(half):
            for r in range(4):
                scale_mask_row(half, r)
            nc.scalar.copy(
                out=mt[half][:].rearrange("p (n i) r -> p n r i", i=4),
                in_=mt_rows[:].rearrange("p r (n i) -> p n r i", i=4),
            )

        def sigmoid(h, first=0):
            nc.scalar.activation(out=gate[h][:, first:], in_=og_raw[h][:, first:], func=ACT.Sigmoid)

        def bank_of(h, c):
            return score_banks[h % 2][(4 * (h // 2) + c) % 3]

        def score_pass(h, c, r):
            a, g = divmod(h, 2)
            rows = slice(ROWS * g, ROWS * (g + 1))
            tokens = slice(P * r, P * (r + 1))
            queries = slice(P * c, P * (c + 1))
            nc.tensor.matmul_mx(
                out=bank_of(h, c)[:, r, :],
                lhsT=k_mx[a][1][rows, tokens].bitcast(FP8X4),
                lhsT_scale=k_mx[a][2][rows, tokens],
                rhs=q_mx[a][1][rows, queries].bitcast(FP8X4),
                rhs_scale=q_mx[a][2][rows, queries],
                start=True,
                stop=True,
            )

        def scores(h, c):
            for r in range(4):
                score_pass(h, c, r)

        def scores_side_by_side(first, second):
            for r in range(4):
                score_pass(first[0], first[1], r)
                score_pass(second[0], second[1], r)

        def weights(h, c):
            run = RUN[h]
            count = P // run
            group, place = divmod(c, run)
            dst = w_mx[h][0][:].rearrange("p (g x s r) -> p g x s r", x=run, s=P, r=4)
            queries = slice(P * (c % 2), P * (c % 2 + 1))
            nc.vector.tensor_tensor(
                out=dst[:, group, :, count * place : count * (place + 1)],
                in0=bank_of(h, c)[:].rearrange("p r (s x) -> p x s r", x=run),
                in1=mt[c // 2][:, queries].rearrange("p (s x) r -> p x s r", x=run),
                op=MULT,
            )

        def values_product(h, c0, c1, bank):
            a, g = divmod(h, 2)
            cols = slice(E * g, E * (g + 1))
            for c in range(c0, c1):
                words = slice(P * c, P * (c + 1))
                nc.tensor.matmul_mx(
                    out=y_banks[bank][:, E * c : E * (c + 1)],
                    lhsT=w_mx[h][1][:, words].bitcast(FP8X4),
                    lhsT_scale=w_mx[h][2][:, words],
                    rhs=v_mx[a][1][:, cols].bitcast(FP8X4),
                    rhs_scale=v_mx[a][2][:, cols],
                    start=True,
                    stop=True,
                )

        def gated(h, c0, c1, bank):
            cols = slice(E * c0, E * c1)
            nc.vector.scalar_tensor_tensor(
                out=res[h][:, cols], in0=y_banks[bank][:, cols], scalar=1.0 / 16.0, in1=gate[h][:, cols], op0=MULT, op1=MULT
            )

        def store(h, group):
            width = RUN[h] * E
            nc.sync.dma_start(out=rows_of(out, h)[:, group], in_=res[h][:, width * group : width * (group + 1)])

        nc.scalar.dma_start(out=og_first[:], in_=rows_of(og, 0)[:, 0, 0:EARLY])
        nc.scalar.dma_start(out=t_sb[:], in_=t.rearrange("(p r) o -> p (r o)", r=4))
        nc.scalar.activation(out=gate[0][:, 0:EARLY], in_=og_first[:], func=ACT.Sigmoid)
        load_features(k_raw, k_rows, 0)
        load_features(q_raw, q_rows, 0)
        for r0 in (0, 2):
            nc.sync.dma_start(out=m_raw[:, r0 : r0 + 2], in_=mask.rearrange("(p r) w -> p r w", r=4)[:, r0 : r0 + 2])
        load_features(k_raw, k_rows, 1)
        load_features(q_raw, q_rows, 1)
        load_v(0)
        load_og(0)
        load_og(1)
        load_v(1)
        load_og(2)
        load_og(3)

        round_k_vector(0, 0, SPLIT)
        round_k_scalar(0, SPLIT, P)
        quantize(k_mx[0], 0, N)
        round_q(nc.vector.tensor_copy, 2, 0, 0)
        round_q(nc.scalar.copy, 4, 0, 1)
        quantize(q_mx[0], 0, 2 * P)
        scores(0, 0)
        scores(1, 0)
        scores_side_by_side((0, 1), (1, 1))
        quantize(q_mx[0], 2 * P, NQ)
        scores_side_by_side((0, 2), (1, 2))
        mask_times_t_vector(0)
        mask_times_t_scalar(1)
        round_k_scalar(1, 0, P)
        round_q(nc.scalar.copy, 4, 1, 0)
        cast_v(0)
        round_q(nc.scalar.copy, 4, 1, 1)
        sigmoid(0, EARLY)
        sigmoid(1)

        weights(0, 0)
        weights(1, 0)
        scores_side_by_side((0, 3), (1, 3))
        for c in range(1, 4):
            weights(0, c)
            weights(1, c)
        quantize(k_mx[1], 0, N)
        quantize(w_mx[0], 0, 2 * P)
        quantize(q_mx[1], 0, 2 * P)
        scores(2, 0)
        scores(3, 0)
        scores_side_by_side((2, 1), (3, 1))
        quantize(w_mx[0], 2 * P, NQ)
        quantize(w_mx[1], 0, NQ)
        weights(2, 0)
        quantize(v_mx[0], 0, 2 * E)
        values_product(0, 0, 4, 0)
        values_product(1, 0, 4, 1)
        weights(3, 0)
        quantize(q_mx[1], 2 * P, NQ)
        scores_side_by_side((2, 2), (3, 2))
        scores_side_by_side((2, 3), (3, 3))
        cast_v(1)
        sigmoid(2)
        sigmoid(3)
        weights(2, 1)
        gated(0, 0, 4, 0)
        store(0, 0)
        weights(3, 1)
        gated(1, 0, 4, 1)
        store(1, 0)
        weights(2, 2)
        quantize(w_mx[3], 0, 2 * P)
        weights(2, 3)
        quantize(v_mx[1], 0, 2 * E)
        values_product(3, 0, 2, 1)
        quantize(w_mx[2], 0, NQ)
        values_product(2, 0, 4, 0)
        weights(3, 2)
        gated(3, 0, 2, 1)
        store(3, 0)
        weights(3, 3)
        quantize(w_mx[3], 2 * P, NQ)
        values_product(3, 2, 4, 1)
        gated(2, 0, 4, 0)
        store(2, 0)
        gated(3, 2, 4, 1)
        store(3, 1)
